import numpy as np
CORES = [0,1,8,9,16,17,24,25,32,33,40,41,48,49,56,57,64,65,72,73,80,81,88,89,96,97,104,105,112,113,120,121,128,129,136,137,144,145,152,153,160,161,168,169,176,177,184,185,192,193,200,201,208,209,216,217,224,225,232,233,240,241,248,249,256,257,264,265,272,273,280,281,288,289,296,297,304,305,312,313,320,321,328,329,336,337,344,345,352,353,360,361,368,369,376,377,384,385,392,393,400,401,408,409,416,417,424,425,432,433,440,441,448,449,456,457,464,465,472,473,480,481,488,489,496,497,504,505]
N = 128
ROUNDS = 8
PERM = [[i, (i + 64) % N] for i in range(N)]
def setup_inputs(rng):
    return {"x": rng.standard_normal((N, ROUNDS, 128, 64), dtype=np.float32)}
def reference(x):
    y = np.empty_like(x)
    for s, d in PERM:
        y[d] = x[s]
    return {"y": y}

from concourse.bass import DstId, RemoteDMATransfer

ROUNDS = 8
PHASES = ROUNDS // 2

SCRATCH = {
    "own": ("dram", [2, 128, 64], "float32"),
    "relay": ("dram", [2, 128, 64], "float32"),
}
SEMAPHORES = ["loaded", "stored", "sent", "passing", "landed"]

LO, HI = 0x0F, 0xF0
PER_CALL = 8


def rank_program(g, core, T, topo):
    if T.rank_of(core) is None:
        return
    h, place = topo.host(core), core % 128

    def at(host):
        return host * 128 + place

    def transfer(dst_core, mask, sem, src, dst):
        rid, pid = topo.addr(dst_core, core)
        return RemoteDMATransfer(dst_ids=[DstId(rid=rid, pnc=pid)], dma_engine_mask=mask, remote_sem=sem,
                                 src=src, dst=dst)

    even_relay, odd_relay = (at(3), at(1)) if h % 2 == 0 else (at(0), at(2))
    side = h // 2
    client0, client1 = (at(1), at(3)) if h % 2 == 0 else (at(0), at(2))
    parity = 0 if h in (0, 3) else 1

    for p in range(PHASES):
        if p:
            g.wait_ge(T.sem.landed, PER_CALL * p)
            g.dma_start(T.y[2 * p - 2:2 * p], T.own[:]).then_inc(T.sem.stored, 16)
            g.wait_ge(T.sem.stored, 16 * p)
        g.dma_start(T.own[:], T.x[2 * p:2 * p + 2]).then_inc(T.sem.loaded, 16)
        g.wait_ge(T.sem.loaded, 16 * (p + 1))
        slot = (side + p) % 2
        g.remote_dma_fused([
            transfer(even_relay, LO, T.sem.passing, T.own[0], T.relay[slot]),
            transfer(odd_relay, HI, T.sem.passing, T.own[1], T.relay[slot]),
        ], local_sem=T.sem.sent)
        g.wait_ge(T.sem.passing, PER_CALL * (p + 1))
        g.remote_dma_fused([
            transfer(client1, LO, T.sem.landed, T.relay[p % 2], T.own[parity]),
            transfer(client0, HI, T.sem.landed, T.relay[(p + 1) % 2], T.own[parity]),
        ], local_sem=T.sem.sent)

    g.wait_ge(T.sem.landed, PER_CALL * PHASES)
    g.dma_start(T.y[ROUNDS - 2:ROUNDS], T.own[:]).then_inc(T.sem.stored, 16)
    g.wait_ge(T.sem.stored, 16 * PHASES)
    g.wait_ge(T.sem.sent, 2 * PER_CALL * PHASES)
